import numpy as np
import ml_dtypes

BF16 = ml_dtypes.bfloat16


def bf(x):
    return np.asarray(x, np.float32).astype(BF16)


def f32(x):
    return np.asarray(x, np.float32)


def f64(x):
    return np.asarray(x).astype(np.float64)


def striped(idx):
    return np.tile(idx.reshape(-1, 16).T, (8, 1))


S, K, M, N = 4096, 128, 128, 4096


def setup_inputs():
    return {"table": bf(np.random.standard_normal((K, S))), "w": bf(np.random.standard_normal((K, M)) / np.sqrt(K)), "offs": striped(np.random.permutation(S))}


def reference(table, w, offs):
    idx = offs[:16].T.reshape(-1)
    x = f64(table)[:, idx]
    y = f64(w).T @ x
    return y

@@ -1,0 +1,33 @@
+import concourse.mybir as mybir
+
+BF16, F32, U16 = mybir.dt.bfloat16, mybir.dt.float32, mybir.dt.uint16
+
+K, M = 128, 128
+S, N = 4096, 4096
+PIECE = 512
+PIECE_COLS = PIECE // 16
+
+FLOPS = 2 * K * M * N
+
+
+def tile_gather_matmul_kernel(tc, table, w, offs, out):
+    nc = tc.nc
+    with (
+        tc.tile_pool(name="held", bufs=1) as held,
+        tc.tile_pool(name="staging", bufs=N // PIECE) as staging,
+        tc.psum_pool(name="banks", bufs=N // PIECE) as banks,
+    ):
+        offsets = held.tile([128, N // 16], U16, name="offsets")
+        nc.sync.dma_start(offsets[:], offs)
+        weights = held.tile([K, M], BF16, name="weights")
+        nc.sync.dma_start(weights[:], w)
+        tokens = held.tile([K, S], BF16, name="tokens")
+        nc.sync.dma_start(tokens[:], table)
+
+        for p in range(N // PIECE):
+            picked = tokens[:].indirect(offsets[:, p * PIECE_COLS : (p + 1) * PIECE_COLS])
+            product = banks.tile([M, PIECE], F32, name="product")
+            nc.tensor.matmul(product[:], weights[:], picked, start=True, stop=True)
+            staged = staging.tile([M, PIECE], F32, name="staged")
+            nc.vector.tensor_copy(staged[:], product[:])
+            nc.sync.dma_start(out[:, p * PIECE : (p + 1) * PIECE], staged[:])

@@ -8,6 +8,7 @@ PIECE = 512
 PIECE_COLS = PIECE // 16
 
 FLOPS = 2 * K * M * N
+WARM_UP = 8
 
 
 def tile_gather_matmul_kernel(tc, table, w, offs, out):
@@ -15,7 +16,8 @@ def tile_gather_matmul_kernel(tc, table, w, offs, out):
     with (
         tc.tile_pool(name="held", bufs=1) as held,
         tc.tile_pool(name="staging", bufs=N // PIECE) as staging,
-        tc.psum_pool(name="banks", bufs=N // PIECE) as banks,
+        tc.psum_pool(name="unread", bufs=1) as unread,
+        tc.psum_pool(name="banks", bufs=4) as banks,
     ):
         offsets = held.tile([128, N // 16], U16, name="offsets")
         nc.sync.dma_start(offsets[:], offs)
@@ -23,6 +25,12 @@ def tile_gather_matmul_kernel(tc, table, w, offs, out):
         nc.sync.dma_start(weights[:], w)
         tokens = held.tile([K, S], BF16, name="tokens")
         nc.sync.dma_start(tokens[:], table)
+
+        zeros = held.tile([K, PIECE], BF16, name="zeros")
+        nc.vector.memset(zeros[:], 0.0)
+        nothing = unread.tile([M, PIECE], F32, name="nothing")
+        for _ in range(WARM_UP):
+            nc.tensor.matmul(nothing[:], zeros[:, :M], zeros[:], start=True, stop=True)
 
         for p in range(N // PIECE):
             picked = tokens[:].indirect(offsets[:, p * PIECE_COLS : (p + 1) * PIECE_COLS])

@@ -8,7 +8,6 @@ PIECE = 512
 PIECE_COLS = PIECE // 16
 
 FLOPS = 2 * K * M * N
-WARM_UP = 8
 
 
 def tile_gather_matmul_kernel(tc, table, w, offs, out):
@@ -16,26 +15,23 @@ def tile_gather_matmul_kernel(tc, table, w, offs, out):
     with (
         tc.tile_pool(name="held", bufs=1) as held,
         tc.tile_pool(name="staging", bufs=N // PIECE) as staging,
-        tc.psum_pool(name="unread", bufs=1) as unread,
-        tc.psum_pool(name="banks", bufs=4) as banks,
+        tc.psum_pool(name="banks", bufs=N // PIECE) as banks,
     ):
         offsets = held.tile([128, N // 16], U16, name="offsets")
-        nc.sync.dma_start(offsets[:], offs)
         weights = held.tile([K, M], BF16, name="weights")
-        nc.sync.dma_start(weights[:], w)
         tokens = held.tile([K, S], BF16, name="tokens")
-        nc.sync.dma_start(tokens[:], table)
-
-        zeros = held.tile([K, PIECE], BF16, name="zeros")
-        nc.vector.memset(zeros[:], 0.0)
-        nothing = unread.tile([M, PIECE], F32, name="nothing")
-        for _ in range(WARM_UP):
-            nc.tensor.matmul(nothing[:], zeros[:, :M], zeros[:], start=True, stop=True)
+        nc.scalar.dma_start(tokens[:], table)
+        nc.sync.dma_start(offsets[:], offs)
+        nc.sync.dma_start(weights[:], w)
 
         for p in range(N // PIECE):
             picked = tokens[:].indirect(offsets[:, p * PIECE_COLS : (p + 1) * PIECE_COLS])
             product = banks.tile([M, PIECE], F32, name="product")
             nc.tensor.matmul(product[:], weights[:], picked, start=True, stop=True)
             staged = staging.tile([M, PIECE], F32, name="staged")
-            nc.vector.tensor_copy(staged[:], product[:])
-            nc.sync.dma_start(out[:, p * PIECE : (p + 1) * PIECE], staged[:])
+            if p % 2 == 0:
+                nc.vector.tensor_copy(staged[:], product[:])
+                nc.sync.dma_start(out[:, p * PIECE : (p + 1) * PIECE], staged[:])
+            else:
+                nc.scalar.copy(staged[:], product[:])
+                nc.scalar.dma_start(out[:, p * PIECE : (p + 1) * PIECE], staged[:])

@@ -4,8 +4,11 @@ BF16, F32, U16 = mybir.dt.bfloat16, mybir.dt.float32, mybir.dt.uint16
 
 K, M = 128, 128
 S, N = 4096, 4096
-PIECE = 512
-PIECE_COLS = PIECE // 16
+BANK = 512
+PSUM_BANKS = 8
+
+WIDTHS = [BANK] * 7 + [256, 128, 128]
+assert sum(WIDTHS) == N
 
 FLOPS = 2 * K * M * N
 
@@ -14,24 +17,22 @@ def tile_gather_matmul_kernel(tc, table, w, offs, out):
     nc = tc.nc
     with (
         tc.tile_pool(name="held", bufs=1) as held,
-        tc.tile_pool(name="staging", bufs=N // PIECE) as staging,
-        tc.psum_pool(name="banks", bufs=N // PIECE) as banks,
+        tc.tile_pool(name="staging", bufs=len(WIDTHS)) as staging,
+        tc.psum_pool(name="banks", bufs=PSUM_BANKS) as banks,
     ):
         offsets = held.tile([128, N // 16], U16, name="offsets")
-        weights = held.tile([K, M], BF16, name="weights")
-        tokens = held.tile([K, S], BF16, name="tokens")
-        nc.scalar.dma_start(tokens[:], table)
         nc.sync.dma_start(offsets[:], offs)
+        weights = held.tile([K, M], BF16, name="weights")
         nc.sync.dma_start(weights[:], w)
+        tokens = held.tile([K, S], BF16, name="tokens")
+        nc.sync.dma_start(tokens[:], table)
 
-        for p in range(N // PIECE):
-            picked = tokens[:].indirect(offsets[:, p * PIECE_COLS : (p + 1) * PIECE_COLS])
-            product = banks.tile([M, PIECE], F32, name="product")
+        first = 0
+        for width in WIDTHS:
+            picked = tokens[:].indirect(offsets[:, first // 16 : (first + width) // 16])
+            product = banks.tile([M, width], F32, name="product")
             nc.tensor.matmul(product[:], weights[:], picked, start=True, stop=True)
-            staged = staging.tile([M, PIECE], F32, name="staged")
-            if p % 2 == 0:
-                nc.vector.tensor_copy(staged[:], product[:])
-                nc.sync.dma_start(out[:, p * PIECE : (p + 1) * PIECE], staged[:])
-            else:
-                nc.scalar.copy(staged[:], product[:])
-                nc.scalar.dma_start(out[:, p * PIECE : (p + 1) * PIECE], staged[:])
+            staged = staging.tile([M, width], F32, name="staged")
+            nc.vector.tensor_copy(staged[:], product[:])
+            nc.sync.dma_start(out[:, first : first + width], staged[:])
+            first += width

@@ -7,7 +7,7 @@ S, N = 4096, 4096
 BANK = 512
 PSUM_BANKS = 8
 
-WIDTHS = [BANK] * 7 + [256, 128, 128]
+WIDTHS = [128, 128, 256] + [BANK] * 7
 assert sum(WIDTHS) == N
 
 FLOPS = 2 * K * M * N

@@ -6,6 +6,7 @@ K, M = 128, 128
 S, N = 4096, 4096
 BANK = 512
 PSUM_BANKS = 8
+BURST = 256
 
 WIDTHS = [128, 128, 256] + [BANK] * 7
 assert sum(WIDTHS) == N
@@ -20,11 +21,11 @@ def tile_gather_matmul_kernel(tc, table, w, offs, out):
         tc.tile_pool(name="staging", bufs=len(WIDTHS)) as staging,
         tc.psum_pool(name="banks", bufs=PSUM_BANKS) as banks,
     ):
-        offsets = held.tile([128, N // 16], U16, name="offsets")
+        offsets = held.tile([128, N // 16], U16, name="offsets", align_bytes=BURST)
         nc.sync.dma_start(offsets[:], offs)
-        weights = held.tile([K, M], BF16, name="weights")
+        weights = held.tile([K, M], BF16, name="weights", align_bytes=BURST)
         nc.sync.dma_start(weights[:], w)
-        tokens = held.tile([K, S], BF16, name="tokens")
+        tokens = held.tile([K, S], BF16, name="tokens", align_bytes=BURST)
         nc.sync.dma_start(tokens[:], table)
 
         first = 0
@@ -32,7 +33,7 @@ def tile_gather_matmul_kernel(tc, table, w, offs, out):
             picked = tokens[:].indirect(offsets[:, first // 16 : (first + width) // 16])
             product = banks.tile([M, width], F32, name="product")
             nc.tensor.matmul(product[:], weights[:], picked, start=True, stop=True)
-            staged = staging.tile([M, width], F32, name="staged")
+            staged = staging.tile([M, width], F32, name="staged", align_bytes=BURST)
             nc.vector.tensor_copy(staged[:], product[:])
             nc.sync.dma_start(out[:, first : first + width], staged[:])
             first += width

@@ -8,7 +8,10 @@ BANK = 512
 PSUM_BANKS = 8
 BURST = 256
 
-WIDTHS = [128, 128, 256] + [BANK] * 7
+RAMP = list(range(128, BANK, 64))
+WHOLE_BANKS = (N - sum(RAMP)) // BANK
+LEFT_OVER = (N - sum(RAMP)) % BANK
+WIDTHS = sorted(RAMP + [LEFT_OVER]) + [BANK] * (WHOLE_BANKS - 1) + [BANK // 2] * 2
 assert sum(WIDTHS) == N
 
 FLOPS = 2 * K * M * N

@@ -24,6 +24,10 @@ def tile_gather_matmul_kernel(tc, table, w, offs, out):
         tc.tile_pool(name="staging", bufs=len(WIDTHS)) as staging,
         tc.psum_pool(name="banks", bufs=PSUM_BANKS) as banks,
     ):
+        spark = held.tile([M, 2], F32, name="spark")
+        nc.vector.memset(spark[:], 0.0)
+        nc.scalar.copy(spark[:, 1:2], spark[:, 0:1])
+
         offsets = held.tile([128, N // 16], U16, name="offsets", align_bytes=BURST)
         nc.sync.dma_start(offsets[:], offs)
         weights = held.tile([K, M], BF16, name="weights", align_bytes=BURST)
@@ -32,11 +36,14 @@ def tile_gather_matmul_kernel(tc, table, w, offs, out):
         nc.sync.dma_start(tokens[:], table)
 
         first = 0
-        for width in WIDTHS:
+        for piece, width in enumerate(WIDTHS):
             picked = tokens[:].indirect(offsets[:, first // 16 : (first + width) // 16])
             product = banks.tile([M, width], F32, name="product")
             nc.tensor.matmul(product[:], weights[:], picked, start=True, stop=True)
             staged = staging.tile([M, width], F32, name="staged", align_bytes=BURST)
-            nc.vector.tensor_copy(staged[:], product[:])
+            if piece % 2 == 0:
+                nc.scalar.copy(staged[:], product[:])
+            else:
+                nc.vector.tensor_copy(staged[:], product[:])
             nc.sync.dma_start(out[:, first : first + width], staged[:])
             first += width

@@ -8,10 +8,10 @@ BANK = 512
 PSUM_BANKS = 8
 BURST = 256
 
-RAMP = list(range(128, BANK, 64))
-WHOLE_BANKS = (N - sum(RAMP)) // BANK
-LEFT_OVER = (N - sum(RAMP)) % BANK
-WIDTHS = sorted(RAMP + [LEFT_OVER]) + [BANK] * (WHOLE_BANKS - 1) + [BANK // 2] * 2
+PIECE = 3 * BANK // 4
+END = PIECE // 2
+WHOLE, LEFT_OVER = divmod(N - 2 * END, PIECE)
+WIDTHS = [END, LEFT_OVER] + [PIECE] * WHOLE + [END]
 assert sum(WIDTHS) == N
 
 FLOPS = 2 * K * M * N

import concourse.mybir as mybir

BF16, F32, U16 = mybir.dt.bfloat16, mybir.dt.float32, mybir.dt.uint16

K, M = 128, 128
S, N = 4096, 4096
BANK = 512
PSUM_BANKS = 8
BURST = 256

PIECE = 3 * BANK // 4
END = PIECE // 2
WHOLE, LEFT_OVER = divmod(N - 2 * END, PIECE)
WIDTHS = [END, LEFT_OVER] + [PIECE] * WHOLE + [END]
assert sum(WIDTHS) == N

FLOPS = 2 * K * M * N


def tile_gather_matmul_kernel(tc, table, w, offs, out):
    nc = tc.nc
    with (
        tc.tile_pool(name="held", bufs=1) as held,
        tc.tile_pool(name="staging", bufs=len(WIDTHS)) as staging,
        tc.psum_pool(name="banks", bufs=PSUM_BANKS) as banks,
    ):
        spark = held.tile([M, 2], F32, name="spark")
        nc.vector.memset(spark[:], 0.0)
        nc.scalar.copy(spark[:, 1:2], spark[:, 0:1])

        offsets = held.tile([128, N // 16], U16, name="offsets", align_bytes=BURST)
        nc.sync.dma_start(offsets[:], offs)
        weights = held.tile([K, M], BF16, name="weights", align_bytes=BURST)
        nc.sync.dma_start(weights[:], w)
        tokens = held.tile([K, S], BF16, name="tokens", align_bytes=BURST)
        nc.sync.dma_start(tokens[:], table)

        first = 0
        for piece, width in enumerate(WIDTHS):
            picked = tokens[:].indirect(offsets[:, first // 16 : (first + width) // 16])
            product = banks.tile([M, width], F32, name="product")
            nc.tensor.matmul(product[:], weights[:], picked, start=True, stop=True)
            staged = staging.tile([M, width], F32, name="staged", align_bytes=BURST)
            if piece % 2 == 0:
                nc.scalar.copy(staged[:], product[:])
            else:
                nc.vector.tensor_copy(staged[:], product[:])
            nc.sync.dma_start(out[:, first : first + width], staged[:])
            first += width
